import numpy as np
import ml_dtypes


def mxq(x, axis, fmt="e4m3"):
    dtype, down = {"e4m3": (ml_dtypes.float8_e4m3fn, 7), "e5m2": (ml_dtypes.float8_e5m2, 14)}[fmt]
    v = np.moveaxis(np.asarray(x, np.float32).astype(ml_dtypes.bfloat16).astype(np.float64), axis, -1)
    blocks = v.reshape(v.shape[:-1] + (-1, 32))
    amax = np.abs(blocks).max(-1, keepdims=True)
    byte = np.maximum(np.where(amax > 0, np.frexp(amax)[1] - 1 + 127, 0) - down, 1)
    scale = np.exp2(byte - 127.0)
    codes = (blocks / scale).astype(np.float32).astype(dtype).astype(np.float64)
    return np.moveaxis((codes * scale).reshape(v.shape), -1, axis)


WIDE = False


def mx_kscale(k):
    if not WIDE:
        return np.ones(k)
    levels = np.array([10, -10, 5, -5, 0])
    if k % 512:
        return np.exp2(np.random.permutation(np.resize(levels, k // 32))).repeat(32)
    a = np.empty((k // 512, 16))
    for p in range(k // 512):
        a[p, :8] = np.random.permutation(np.resize(levels, 8))
        for g in range(8):
            far = levels[np.abs(levels - a[p, g]) >= 10]
            a[p, g + 8] = far[np.random.randint(len(far))]
    return np.exp2(a.ravel()).repeat(32)


BF16 = ml_dtypes.bfloat16


def bf(x):
    return np.asarray(x, np.float32).astype(BF16)


def f64(x):
    return np.asarray(x).astype(np.float64)


E2M1 = np.array([0.0, 0.5, 1.0, 1.5, 2.0, 3.0, 4.0, 6.0, -0.0, -0.5, -1.0, -1.5, -2.0, -3.0, -4.0, -6.0])


def pack_weight(w, fmt):
    k, n = w.shape
    w = f64(bf(w)).reshape(k // 32, 32, n)
    amax = np.abs(w).max(1)
    if fmt == "e4m3":
        byte = np.frexp(amax)[1] - 1 + 127 - 7
    else:
        mant, ex = np.frexp(amax / 6.0)
        byte = np.where(mant > 0.5, ex, ex - 1) + 127
    byte = np.clip(np.where(amax > 0, byte, 1), 1, 254)
    scaled = (w * np.exp2(127.0 - byte)[:, None, :]).reshape(k, n).astype(np.float32)
    by_word = np.ascontiguousarray(scaled.reshape(k // 512, 128, 4, n).transpose(0, 1, 3, 2))
    if fmt == "e4m3":
        words = by_word.astype(ml_dtypes.float8_e4m3fn).view(np.uint8)
    else:
        c = by_word.astype(ml_dtypes.float4_e2m1fn).view(np.uint8) & 0xF
        words = c[..., 0::2] | (c[..., 1::2] << 4)
    return np.ascontiguousarray(words), np.ascontiguousarray(byte.astype(np.uint8).reshape(k // 512, 16, n))


def unpack_weight(words, scales, fmt):
    g, p, n, _ = words.shape
    if fmt == "e4m3":
        vals = np.ascontiguousarray(words).view(ml_dtypes.float8_e4m3fn).astype(np.float64)
    else:
        nib = np.empty((g, p, n, 4), np.uint8)
        nib[..., 0::2] = words & 0xF
        nib[..., 1::2] = words >> 4
        vals = E2M1[nib]
    vals = vals * np.repeat(np.exp2(scales.astype(np.float64) - 127.0), 8, axis=1)[..., None]
    return vals.transpose(0, 1, 3, 2).reshape(g * 512, n)
def pack4(w):
    words, scales = pack_weight(w, "e2m1")
    return words.reshape(words.shape[0], 128, -1), scales


def unpack4(words, scales):
    return unpack_weight(words.reshape(words.shape[0], 128, -1, 2), scales, "e2m1")


def planes(Y):
    n, m = Y.shape
    b = f64(bf(Y)).reshape(n // 32, 32, m)
    amax = np.abs(b).max(1)
    byte = np.clip(np.where(amax > 0, np.frexp(amax)[1] - 1 + 127 - 7, 1), 1, 254)
    codes = (b * np.exp2(127.0 - byte)[:, None, :]).reshape(n, m).astype(np.float32).astype(ml_dtypes.float8_e4m3fn).view(np.uint8)
    words = codes.reshape(n // 512, 128, 4, m).transpose(0, 1, 3, 2)
    return np.ascontiguousarray(words), np.ascontiguousarray(byte.astype(np.uint8).reshape(n // 512, 16, m))


M, K, N = 768, 1024, 1536
CORR = 0.35


def setup_inputs():
    rn = np.random.randn
    s, t, u = mx_kscale(K), mx_kscale(K), mx_kscale(K)
    x = rn(M, K) * s[None, :]
    w = CORR * rn(K, K) / np.sqrt(K) / s[:, None] * t[None, :]
    w_diag = (1 + 0.1 * rn(K)) * t / s
    d = CORR * rn(K, K) / np.sqrt(K) / t[:, None] * u[None, :]
    d_diag = (1 + 0.1 * rn(K)) * u / t
    fin = rn(K, N) / np.sqrt(K) / u[:, None]
    rest = 0.4 * rn(M, N)
    gain = np.exp(0.8 * rn(N))
    d_words, d_scales = pack4(d)
    return {"x": bf(x), "w": bf(w), "w_diag": bf(w_diag), "d_words": d_words, "d_scales": d_scales,
            "d_diag": bf(d_diag), "fin": bf(fin), "rest": bf(rest), "gain": bf(gain)}


def reference(x, w, w_diag, d_words, d_scales, d_diag, fin, rest, gain):
    x, w, fin = f64(x), f64(w), f64(fin)
    x1 = x * f64(w_diag) + (mxq(x, 1, "e4m3") @ mxq(w, 0, "e4m3"))
    x2 = x1 * f64(d_diag) + (mxq(x1, 1, "e4m3") @ unpack4(d_words, d_scales))
    y = ((mxq(x2, 1, "e4m3") @ mxq(fin, 0, "e4m3")) + f64(rest)) * f64(gain)
    Y = y.T
    words, scales = planes(Y)
    return y, words, scales

@@ -1,0 +1,382 @@
+from contextlib import ExitStack
+
+import concourse.mybir as mybir
+from concourse.masks import make_identity
+
+M, K, N = 768, 1024, 1536
+FLOPS = 2 * M * K * (K + K + N)
+
+F32 = mybir.dt.float32
+BF16 = mybir.dt.bfloat16
+U32 = mybir.dt.uint32
+I32 = mybir.dt.int32
+U8 = mybir.dt.uint8
+FP8X4 = mybir.dt.float8_e4m3fn_x4
+FP4X4 = mybir.dt.float4_e2m1fn_x4
+ADD = mybir.AluOpType.add
+MULT = mybir.AluOpType.mult
+
+P = 128
+PACK = 4
+GROUP = P * PACK
+KG = K // GROUP
+NG = N // GROUP
+CHUNK = 256
+CHUNKS = M // CHUNK
+TILES = M // P
+HALF = GROUP // 2
+
+
+def tile_displaced_overlap_table_k1_kernel(
+    tc, x, w, w_diag, d_words, d_scales, d_diag, fin, rest, gain, out_0, out_1, out_2
+):
+    nc = tc.nc
+    with ExitStack() as ctx:
+        keep = ctx.enter_context(tc.tile_pool(name="keep", bufs=1))
+        ring = ctx.enter_context(tc.tile_pool(name="ring", bufs=2))
+        psum = ctx.enter_context(tc.psum_pool(name="psum", bufs=1))
+        ctx.enter_context(tc.manual_schedule())
+
+        def kept(name, shape, dtype):
+            return keep.tile(shape, dtype, name=name, align_bytes=64)
+
+        def mx_tiles(name, width):
+            return kept(name + "_codes", [P, width], U32), kept(name + "_scales", [P, width], U8)
+
+        def grouped_tile(name):
+            return ring.tile([P, 4 * CHUNK], BF16, name=name, tag="grouped", bufs=6, align_bytes=64)
+
+        def acc_bank(name):
+            return psum.tile([P, GROUP], F32, name=name, tag="acc", bufs=6)
+
+        def turn_bank(name):
+            return psum.tile([P, 4, P], F32, name=name, tag="turn", bufs=2)
+
+        def copy_on(engine, out, in_):
+            if engine == "vector":
+                nc.vector.tensor_copy(out=out, in_=in_)
+            else:
+                nc.scalar.copy(out=out, in_=in_)
+
+        def quantize(mx, cols, src):
+            nc.vector.quantize_mx(out=mx[0][:, cols].bitcast(FP8X4), scales=mx[1][:, cols], in_=src[:])
+
+        ident = kept("ident", [P, P], F32)
+        x_raw = [kept("x_raw%d" % i, [P, K], BF16) for i in range(TILES)]
+        w_raw = {(g, n): kept("w_raw%d%d" % (g, n), [P, PACK, GROUP], BF16) for g in range(KG) for n in range(KG)}
+        f_raw = {(g, n): kept("f_raw%d%d" % (g, n), [P, PACK, GROUP], BF16) for g in range(KG) for n in range(NG)}
+        d_raw = [kept("d_raw%d" % g, [P, 2 * K], U8) for g in range(KG)]
+        ds_raw = kept("ds_raw", [P, KG, K], U8)
+        d_codes = [kept("d_codes%d" % g, [P, 2 * K], U8) for g in range(KG)]
+        ds = kept("ds", [P, KG * K], U8)
+        wd = kept("wd", [P, KG, PACK], BF16)
+        dd = kept("dd", [P, KG, PACK], BF16)
+        rest_sb = [kept("rest%d" % n, [P, TILES, GROUP], BF16) for n in range(NG)]
+        gain_sb = kept("gain_sb", [P, N], BF16)
+        x_t = [kept("x_t%d" % c, [P, KG, CHUNK, PACK], BF16) for c in range(CHUNKS)]
+        x_mx = [mx_tiles("x%d" % c, KG * CHUNK) for c in range(CHUNKS)]
+        w_mx = {key: mx_tiles("w%d%d" % key, GROUP) for key in w_raw}
+        f_mx = {key: mx_tiles("f%d%d" % key, GROUP) for key in f_raw}
+        x1 = {(c, g): kept("x1_%d%d" % (c, g), [P, PACK, CHUNK], F32) for c in range(CHUNKS) for g in range(KG)}
+        x1_mx = {key: mx_tiles("x1_%d%d" % key, CHUNK) for key in x1}
+        x2_mx = {key: mx_tiles("x2_%d%d" % key, CHUNK) for key in x1}
+        y_codes = [kept("y_codes%d" % n, [P, M], U32) for n in range(NG)]
+        y_scales = [kept("y_scales%d" % n, [P, M], U8) for n in range(NG)]
+
+        def load_rows(dst, src, g, n):
+            rows = src[g * GROUP : (g + 1) * GROUP, n * GROUP : (n + 1) * GROUP]
+            nc.sync.dma_start(out=dst[:], in_=rows.rearrange("(p j) c -> p j c", j=PACK))
+
+        def load_x(i):
+            nc.sync.dma_start(out=x_raw[i][:], in_=x[i * P : (i + 1) * P, :])
+
+        def load_d(g):
+            nc.sync.dma_start(out=d_raw[g][:].bitcast(I32), in_=d_words[g].bitcast(I32))
+
+        def load_rest(n):
+            cols = rest[:, n * GROUP : (n + 1) * GROUP]
+            nc.sync.dma_start(out=rest_sb[n][:], in_=cols.rearrange("(i p) c -> p i c", p=P))
+
+        make_identity(nc, ident[:])
+        nc.vector.memset(ds_raw[:].rearrange("p g n -> p (g n)").bitcast(I32), 0)
+        for q in range(4):
+            nc.gpsimd.dma_start(
+                out=ds_raw[32 * q : 32 * q + 4, :, :].bitcast(I32),
+                in_=d_scales[:, 4 * q : 4 * q + 4, :].rearrange("g r n -> r g n").bitcast(I32),
+            )
+        load_d(0)
+        load_x(0)
+        load_rows(w_raw[0, 0], w, 0, 0)
+        load_x(1)
+        load_d(1)
+        load_rows(w_raw[1, 0], w, 1, 0)
+        load_x(2)
+        load_x(3)
+        nc.sync.dma_start(out=wd[:], in_=w_diag.rearrange("(g p t) -> p g t", p=P, t=PACK))
+        load_rows(w_raw[0, 1], w, 0, 1)
+        load_rows(w_raw[1, 1], w, 1, 1)
+        load_x(4)
+        load_x(5)
+        nc.sync.dma_start(out=dd[:], in_=d_diag.rearrange("(g p t) -> p g t", p=P, t=PACK))
+        for n in range(2):
+            for g in range(KG):
+                load_rows(f_raw[g, n], fin, g, n)
+        load_rest(0)
+        nc.sync.dma_start(out=gain_sb[:], in_=gain.partition_broadcast(P))
+        for g in range(KG):
+            load_rows(f_raw[g, 2], fin, g, 2)
+        load_rest(1)
+        load_rest(2)
+
+        staged = {}
+
+        def order_d(g):
+            nc.vector.tensor_copy(
+                out=d_codes[g][:].rearrange("p (n t m b) -> p n t m b", n=KG, t=PACK, b=2),
+                in_=d_raw[g][:].rearrange("p (n m t b) -> p n t m b", n=KG, t=PACK, b=2),
+            )
+
+        def order_d_scales():
+            nc.vector.tensor_copy(
+                out=ds[:].rearrange("p (h t m) -> p h t m", t=PACK, m=P),
+                in_=ds_raw[:].rearrange("p g (n m t) -> p (g n) t m", t=PACK, m=P),
+            )
+
+        def turn_x(i):
+            words = x_raw[i][:].bitcast(F32)
+            bank = turn_bank("x_bank%d" % i)
+            for g in range(KG):
+                for u in range(2):
+                    nc.tensor.transpose(bank[:, 2 * g + u, :], words[:, HALF * g + u : HALF * (g + 1) : 2], ident[:])
+            c, a = divmod(i, 2)
+            dst = x_t[c][:].rearrange("p g m t -> p (g m t)").bitcast(F32).rearrange("p (g m u) -> p g m u", g=KG, u=2)
+            nc.scalar.copy(out=dst[:, :, a * P : (a + 1) * P, :], in_=bank[:].rearrange("p (g u) m -> p g m u", u=2))
+
+        def quantize_x(c):
+            nc.vector.quantize_mx(
+                out=x_mx[c][0][:].bitcast(FP8X4), scales=x_mx[c][1][:], in_=x_t[c][:].rearrange("p g m t -> p (g m t)")
+            )
+
+        def group_w(engine, g, n, h):
+            dst = grouped_tile("w_grouped%d%d%d" % (g, n, h))
+            src = w_raw[g, n][:].rearrange("p j (m t) -> p m j t", t=PACK)[:, :, :, 2 * h : 2 * h + 2]
+            copy_on(engine, dst[:].rearrange("p (t m j) -> p m j t", t=2, j=PACK), src)
+            staged["w", g, n, h] = dst
+
+        def quantize_w(g, n, h):
+            quantize(w_mx[g, n], slice(h * HALF, (h + 1) * HALF), staged.pop(("w", g, n, h)))
+
+        def interleave(engine, dst, src):
+            copy_on(
+                engine,
+                dst[:].rearrange("p (c i t) -> p c t i", i=4, t=PACK),
+                src.rearrange("p t (c i) -> p c t i", i=4),
+            )
+
+        def group_fin(engine, g, n, h):
+            dst = grouped_tile("f_grouped%d%d%d" % (g, n, h))
+            interleave(engine, dst, f_raw[g, n][:, :, h * HALF : (h + 1) * HALF])
+            staged["f", g, n, h] = dst
+
+        def quantize_fin(g, n, h):
+            quantize(f_mx[g, n], slice(h * HALF, (h + 1) * HALF), staged.pop(("f", g, n, h)))
+
+        def multiply_block(stage, c, n):
+            banks = []
+            for pair in range(2):
+                bank = acc_bank("acc%d_%d%d%d" % (stage, c, n, pair))
+                banks.append(bank)
+                for e in range(2):
+                    t = 2 * pair + e
+                    if stage == 1:
+                        for g in range(KG):
+                            cols = slice(g * CHUNK, (g + 1) * CHUNK)
+                            nc.tensor.matmul_mx(
+                                out=bank[:, e * CHUNK : (e + 1) * CHUNK],
+                                lhsT=w_mx[g, n][0][:, t * P : (t + 1) * P].bitcast(FP8X4),
+                                lhsT_scale=w_mx[g, n][1][:, t * P : (t + 1) * P],
+                                rhs=x_mx[c][0][:, cols].bitcast(FP8X4),
+                                rhs_scale=x_mx[c][1][:, cols],
+                                start=(g == 0),
+                                stop=(g == KG - 1),
+                            )
+                    else:
+                        col0 = n * GROUP + t * P
+                        for a in range(2):
+                            for g in range(KG):
+                                nc.tensor.matmul_mx(
+                                    out=bank[:, e * CHUNK + a * P : e * CHUNK + (a + 1) * P],
+                                    lhsT=d_codes[g][:, 2 * col0 : 2 * (col0 + P)].bitcast(FP4X4),
+                                    lhsT_scale=ds[:, g * K + col0 : g * K + col0 + P],
+                                    rhs=x1_mx[c, g][0][:, a * P : (a + 1) * P].bitcast(FP8X4),
+                                    rhs_scale=x1_mx[c, g][1][:, a * P : (a + 1) * P],
+                                    start=(g == 0),
+                                    stop=(g == KG - 1),
+                                )
+            staged["acc", stage, c, n] = banks
+
+        def add_diagonal(stage, c, n):
+            banks = staged.pop(("acc", stage, c, n))
+            if stage == 1:
+                dst = x1[c, n]
+            else:
+                dst = ring.tile([P, PACK, CHUNK], BF16, name="x2_%d%d" % (c, n), tag="x2", bufs=3)
+            for t in range(PACK):
+                pair, e = divmod(t, 2)
+                nc.vector.scalar_tensor_tensor(
+                    out=dst[:, t, :],
+                    in0=x_t[c][:, n, :, t] if stage == 1 else x1[c, n][:, t, :],
+                    scalar=(wd if stage == 1 else dd)[:, n, t : t + 1],
+                    in1=banks[pair][:, e * CHUNK : (e + 1) * CHUNK],
+                    op0=MULT,
+                    op1=ADD,
+                )
+            staged["slots", stage, c, n] = dst
+
+        def group_block(stage, c, n):
+            dst = grouped_tile("x_grouped%d_%d%d" % (stage, c, n))
+            interleave("scalar", dst, staged.pop(("slots", stage, c, n))[:])
+            staged["grouped", stage, c, n] = dst
+
+        def quantize_block(stage, c, n):
+            mx = x1_mx if stage == 1 else x2_mx
+            quantize(mx[c, n], slice(0, CHUNK), staged.pop(("grouped", stage, c, n)))
+
+        def multiply_unit(n, i):
+            bank = acc_bank("acc3_%d%d" % (n, i))
+            c, a = divmod(i, 2)
+            for g in range(KG):
+                nc.tensor.matmul_mx(
+                    out=bank[:],
+                    lhsT=x2_mx[c, g][0][:, a * P : (a + 1) * P].bitcast(FP8X4),
+                    lhsT_scale=x2_mx[c, g][1][:, a * P : (a + 1) * P],
+                    rhs=f_mx[g, n][0][:].bitcast(FP8X4),
+                    rhs_scale=f_mx[g, n][1][:],
+                    start=(g == 0),
+                    stop=(g == KG - 1),
+                )
+            staged["acc3", n, i] = bank
+
+        def add_rest(n, i):
+            y = ring.tile([P, GROUP], F32, name="y%d%d" % (n, i), tag="y", bufs=8)
+            nc.vector.tensor_tensor(out=y[:], in0=staged.pop(("acc3", n, i))[:], in1=rest_sb[n][:, i, :], op=ADD)
+            staged["y", n, i] = y
+
+        def weigh(n, i):
+            y = staged.pop(("y", n, i))
+            cols = slice(n * GROUP, (n + 1) * GROUP)
+            y_bf = ring.tile([P, GROUP], BF16, name="y_bf%d%d" % (n, i), tag="y_bf", bufs=4)
+            sorted_out = y_bf[:].rearrange("m (u p e) -> m u p e", u=2, e=2)
+            last = (n, i) == (NG - 1, TILES - 1)
+            if last:
+                nc.vector.tensor_tensor(
+                    out=sorted_out,
+                    in0=y[:].rearrange("m (p u e) -> m u p e", u=2, e=2),
+                    in1=gain_sb[:, cols].rearrange("m (p u e) -> m u p e", u=2, e=2),
+                    op=MULT,
+                )
+            nc.vector.tensor_tensor(out=y[:], in0=y[:], in1=gain_sb[:, cols], op=MULT)
+            nc.sync.dma_start(out=out_0[i * P : (i + 1) * P, cols], in_=y[:])
+            if not last:
+                nc.scalar.copy(out=sorted_out, in_=y[:].rearrange("m (p u e) -> m u p e", u=2, e=2))
+            staged["y_bf", n, i] = y_bf
+
+        def turn_y(n, tiles):
+            bank = turn_bank("y_bank%d%d" % (n, tiles[0]))
+            for a, i in enumerate(tiles):
+                words = staged.pop(("y_bf", n, i))[:].bitcast(F32)
+                for u in range(2):
+                    nc.tensor.transpose(bank[:, 2 * a + u, :], words[:, u * P : (u + 1) * P], ident[:])
+            staged["y_bank", n, tiles] = bank
+
+        def group_y(n, tiles):
+            dst = grouped_tile("y_grouped%d%d" % (n, tiles[0]))
+            width = len(tiles) * GROUP
+            nc.scalar.copy(
+                out=dst[:, :width].bitcast(F32).rearrange("p (a m u) -> p a m u", m=P, u=2),
+                in_=staged.pop(("y_bank", n, tiles))[:, : 2 * len(tiles), :].rearrange("p (a u) m -> p a m u", u=2),
+            )
+            staged["y_grouped", n, tiles] = dst[:, :width]
+
+        def quantize_y(n, tiles):
+            cols = slice(tiles[0] * P, (tiles[-1] + 1) * P)
+            quantize((y_codes[n], y_scales[n]), cols, staged.pop(("y_grouped", n, tiles)))
+            words = out_1[n].rearrange("p m t -> p (m t)").bitcast(I32)
+            nc.sync.dma_start(out=words[:, cols], in_=y_codes[n][:, cols].bitcast(I32))
+            if tiles[-1] == TILES - 1:
+                for q in range(4):
+                    queue = nc.scalar if n == NG - 1 and q % 2 == 1 else nc.sync
+                    queue.dma_start(
+                        out=out_2[n, 4 * q : 4 * q + 4, :].bitcast(I32),
+                        in_=y_scales[n][32 * q : 32 * q + 4, :].bitcast(I32),
+                    )
+
+        blocks = [(1, 0, 0), (1, 1, 0), (1, 0, 1), (1, 1, 1), (1, 2, 0), (1, 2, 1)]
+        blocks = blocks + [(2, c, n) for c in range(CHUNKS) for n in range(KG)]
+        units = [(n, i) for n in range(NG) for i in range(TILES)]
+        fin_items = [(g, n, h) for n in range(NG) for g in range(KG) for h in range(2)]
+
+        order_d(0)
+        turn_x(0)
+        group_w("scalar", 0, 0, 1)
+        group_w("vector", 0, 0, 0)
+        turn_x(1)
+        order_d_scales()
+        quantize_w(0, 0, 0)
+        group_w("scalar", 1, 0, 1)
+        quantize_w(0, 0, 1)
+        quantize_x(0)
+        group_w("vector", 1, 0, 0)
+        turn_x(2)
+        turn_x(3)
+        order_d(1)
+        quantize_w(1, 0, 0)
+        quantize_w(1, 0, 1)
+        multiply_block(*blocks[0])
+        group_w("scalar", 0, 1, 1)
+        quantize_x(1)
+        group_w("vector", 0, 1, 0)
+        group_w("scalar", 1, 1, 1)
+        turn_x(4)
+        turn_x(5)
+        multiply_block(*blocks[1])
+        group_w("vector", 1, 1, 0)
+        quantize_w(0, 1, 0)
+        quantize_w(0, 1, 1)
+        quantize_w(1, 1, 0)
+
+        fin_at = {2: 0, 4: 1, 5: 2, 7: 3, 10: 4, 12: 5, 13: 6, 14: 7, 16: 8, 17: 9, 19: 10, 20: 11}
+        fin_on_vector = (1, 4, 8)
+        nb = len(blocks)
+        turns = {TILES * n + i + 1: (n, (i, i + 1)) for n in range(NG) for i in range(0, TILES, 2)}
+        turns[len(units) - 2] = (NG - 1, (TILES - 2,))
+        turns[len(units) - 1] = (NG - 1, (TILES - 1,))
+        for s in range(nb + len(units) + 5):
+            if 2 <= s + 1 < nb:
+                multiply_block(*blocks[s + 1])
+            if s < nb:
+                add_diagonal(*blocks[s])
+                group_block(*blocks[s])
+            if s == 0:
+                quantize_w(1, 1, 1)
+            if s == 1:
+                quantize_x(2)
+            if s in fin_at:
+                group_fin("vector" if fin_at[s] in fin_on_vector else "scalar", *fin_items[fin_at[s]])
+            if s - 2 in fin_at:
+                quantize_fin(*fin_items[fin_at[s - 2]])
+            if 0 <= s - 2 < nb:
+                quantize_block(*blocks[s - 2])
+            u = s - nb
+            if u - 3 in turns:
+                turn_y(*turns[u - 3])
+            if 0 <= u + 2 < len(units):
+                multiply_unit(*units[u + 2])
+            if 0 <= u < len(units):
+                add_rest(*units[u])
+            if u - 5 in turns:
+                quantize_y(*turns[u - 5])
+            if u - 3 in turns:
+                group_y(*turns[u - 3])
+            if 0 <= u - 1 < len(units):
+                weigh(*units[u - 1])

@@ -25,6 +25,7 @@ CHUNK = 256
 CHUNKS = M // CHUNK
 TILES = M // P
 HALF = GROUP // 2
+GPSIMD_ROWS = 96
 
 
 def tile_displaced_overlap_table_k1_kernel(
@@ -44,10 +45,10 @@ def tile_displaced_overlap_table_k1_kernel(
             return kept(name + "_codes", [P, width], U32), kept(name + "_scales", [P, width], U8)
 
         def grouped_tile(name):
-            return ring.tile([P, 4 * CHUNK], BF16, name=name, tag="grouped", bufs=6, align_bytes=64)
+            return ring.tile([P, 4 * CHUNK], BF16, name=name, tag="grouped", bufs=8, align_bytes=64)
 
         def acc_bank(name):
-            return psum.tile([P, GROUP], F32, name=name, tag="acc", bufs=6)
+            return psum.tile([P, GROUP], F32, name=name, tag="acc", bufs=4)
 
         def turn_bank(name):
             return psum.tile([P, 4, P], F32, name=name, tag="turn", bufs=2)
@@ -55,6 +56,8 @@ def tile_displaced_overlap_table_k1_kernel(
         def copy_on(engine, out, in_):
             if engine == "vector":
                 nc.vector.tensor_copy(out=out, in_=in_)
+            elif engine == "gpsimd":
+                nc.gpsimd.tensor_scalar(out=out, in0=in_, scalar1=1.0, scalar2=0.0, op0=MULT, op1=ADD)
             else:
                 nc.scalar.copy(out=out, in_=in_)
 
@@ -73,6 +76,8 @@ def tile_displaced_overlap_table_k1_kernel(
         dd = kept("dd", [P, KG, PACK], BF16)
         rest_sb = [kept("rest%d" % n, [P, TILES, GROUP], BF16) for n in range(NG)]
         gain_sb = kept("gain_sb", [P, N], BF16)
+        gain_col = kept("gain_col", [P, NG, PACK], BF16)
+        gain_f32 = kept("gain_f32", [P, NG, PACK], F32)
         x_t = [kept("x_t%d" % c, [P, KG, CHUNK, PACK], BF16) for c in range(CHUNKS)]
         x_mx = [mx_tiles("x%d" % c, KG * CHUNK) for c in range(CHUNKS)]
         w_mx = {key: mx_tiles("w%d%d" % key, GROUP) for key in w_raw}
@@ -81,7 +86,7 @@ def tile_displaced_overlap_table_k1_kernel(
         x1_mx = {key: mx_tiles("x1_%d%d" % key, CHUNK) for key in x1}
         x2_mx = {key: mx_tiles("x2_%d%d" % key, CHUNK) for key in x1}
         y_codes = [kept("y_codes%d" % n, [P, M], U32) for n in range(NG)]
-        y_scales = [kept("y_scales%d" % n, [P, M], U8) for n in range(NG)]
+        y_scales = kept("y_scales", [P, NG, M], U8)
 
         def load_rows(dst, src, g, n):
             rows = src[g * GROUP : (g + 1) * GROUP, n * GROUP : (n + 1) * GROUP]
@@ -99,32 +104,31 @@ def tile_displaced_overlap_table_k1_kernel(
 
         make_identity(nc, ident[:])
         nc.vector.memset(ds_raw[:].rearrange("p g n -> p (g n)").bitcast(I32), 0)
-        for q in range(4):
-            nc.gpsimd.dma_start(
-                out=ds_raw[32 * q : 32 * q + 4, :, :].bitcast(I32),
-                in_=d_scales[:, 4 * q : 4 * q + 4, :].rearrange("g r n -> r g n").bitcast(I32),
-            )
         load_d(0)
         load_x(0)
+        load_d(1)
         load_rows(w_raw[0, 0], w, 0, 0)
         load_x(1)
-        load_d(1)
         load_rows(w_raw[1, 0], w, 1, 0)
         load_x(2)
         load_x(3)
         nc.sync.dma_start(out=wd[:], in_=w_diag.rearrange("(g p t) -> p g t", p=P, t=PACK))
         load_rows(w_raw[0, 1], w, 0, 1)
-        load_rows(w_raw[1, 1], w, 1, 1)
+        for q in range(4):
+            nc.sync.dma_start(
+                out=ds_raw[32 * q : 32 * q + 4, :, :].bitcast(I32),
+                in_=d_scales[:, 4 * q : 4 * q + 4, :].rearrange("g r n -> r g n").bitcast(I32),
+            )
         load_x(4)
         load_x(5)
+        load_rows(w_raw[1, 1], w, 1, 1)
         nc.sync.dma_start(out=dd[:], in_=d_diag.rearrange("(g p t) -> p g t", p=P, t=PACK))
-        for n in range(2):
+        for n in range(NG):
             for g in range(KG):
                 load_rows(f_raw[g, n], fin, g, n)
+        nc.sync.dma_start(out=gain_col[:], in_=gain.rearrange("(n p t) -> p n t", p=P, t=PACK))
         load_rest(0)
         nc.sync.dma_start(out=gain_sb[:], in_=gain.partition_broadcast(P))
-        for g in range(KG):
-            load_rows(f_raw[g, 2], fin, g, 2)
         load_rest(1)
         load_rest(2)
 
@@ -215,13 +219,15 @@ def tile_displaced_overlap_table_k1_kernel(
                                 )
             staged["acc", stage, c, n] = banks
 
-        def add_diagonal(stage, c, n):
-            banks = staged.pop(("acc", stage, c, n))
+        def add_diagonal(stage, c, n, slots):
+            banks = staged["acc", stage, c, n]
             if stage == 1:
                 dst = x1[c, n]
-            else:
+            elif slots[0] == 0:
                 dst = ring.tile([P, PACK, CHUNK], BF16, name="x2_%d%d" % (c, n), tag="x2", bufs=3)
-            for t in range(PACK):
+            else:
+                dst = staged["slots", stage, c, n]
+            for t in slots:
                 pair, e = divmod(t, 2)
                 nc.vector.scalar_tensor_tensor(
                     out=dst[:, t, :],
@@ -233,9 +239,13 @@ def tile_displaced_overlap_table_k1_kernel(
                 )
             staged["slots", stage, c, n] = dst
 
-        def group_block(stage, c, n):
+        def group_block(stage, c, n, shared):
             dst = grouped_tile("x_grouped%d_%d%d" % (stage, c, n))
-            interleave("scalar", dst, staged.pop(("slots", stage, c, n))[:])
+            src = staged.pop(("slots", stage, c, n))
+            rows = GPSIMD_ROWS if shared else 0
+            if shared:
+                interleave("gpsimd", dst[:, : PACK * rows], src[:, :, :rows])
+            interleave("scalar", dst[:, PACK * rows :], src[:, :, rows:])
             staged["grouped", stage, c, n] = dst
 
         def quantize_block(stage, c, n):
@@ -258,28 +268,45 @@ def tile_displaced_overlap_table_k1_kernel(
             staged["acc3", n, i] = bank
 
         def add_rest(n, i):
-            y = ring.tile([P, GROUP], F32, name="y%d%d" % (n, i), tag="y", bufs=8)
+            y = ring.tile([P, GROUP], F32, name="y%d%d" % (n, i), tag="y", bufs=10)
             nc.vector.tensor_tensor(out=y[:], in0=staged.pop(("acc3", n, i))[:], in1=rest_sb[n][:, i, :], op=ADD)
             staged["y", n, i] = y
 
-        def weigh(n, i):
-            y = staged.pop(("y", n, i))
+        def spread_gain(n):
+            bank = psum.tile([P, P, PACK], F32, name="gain_bank%d" % n, tag="gain", bufs=2)
+            for t in range(PACK):
+                nc.tensor.transpose(bank[:, :, t], gain_f32[:, n, t : t + 1].to_broadcast([P, P]), ident[:])
+            staged["gain", n] = bank[:].rearrange("m p t -> m (p t)")
+
+        def weigh(engine, n, i):
+            y = staged["y", n, i]
             cols = slice(n * GROUP, (n + 1) * GROUP)
-            y_bf = ring.tile([P, GROUP], BF16, name="y_bf%d%d" % (n, i), tag="y_bf", bufs=4)
-            sorted_out = y_bf[:].rearrange("m (u p e) -> m u p e", u=2, e=2)
-            last = (n, i) == (NG - 1, TILES - 1)
-            if last:
-                nc.vector.tensor_tensor(
-                    out=sorted_out,
-                    in0=y[:].rearrange("m (p u e) -> m u p e", u=2, e=2),
-                    in1=gain_sb[:, cols].rearrange("m (p u e) -> m u p e", u=2, e=2),
-                    op=MULT,
-                )
-            nc.vector.tensor_tensor(out=y[:], in0=y[:], in1=gain_sb[:, cols], op=MULT)
-            nc.sync.dma_start(out=out_0[i * P : (i + 1) * P, cols], in_=y[:])
-            if not last:
-                nc.scalar.copy(out=sorted_out, in_=y[:].rearrange("m (p u e) -> m u p e", u=2, e=2))
+            if engine == "gpsimd":
+                nc.gpsimd.tensor_tensor(out=y[:], in0=y[:], in1=gain_sb[:, cols], op=MULT)
+            else:
+                nc.vector.tensor_tensor(out=y[:], in0=y[:], in1=staged["gain", n], op=MULT)
+
+        def store_y(n, i):
+            rows = out_0[i * P : (i + 1) * P, n * GROUP : (n + 1) * GROUP]
+            nc.sync.dma_start(out=rows, in_=staged.pop(("y", n, i))[:])
+
+        def sorted_pairs(n, i):
+            y_bf = ring.tile([P, GROUP], BF16, name="y_bf%d%d" % (n, i), tag="y_bf", bufs=6)
             staged["y_bf", n, i] = y_bf
+            return y_bf[:].rearrange("m (u p e) -> m u p e", u=2, e=2)
+
+        def round_y(n, i):
+            y = staged["y", n, i]
+            nc.scalar.copy(out=sorted_pairs(n, i), in_=y[:].rearrange("m (p u e) -> m u p e", u=2, e=2))
+            store_y(n, i)
+
+        def weigh_and_round(n, i):
+            nc.vector.tensor_tensor(
+                out=sorted_pairs(n, i),
+                in0=staged["y", n, i][:].rearrange("m (p u e) -> m u p e", u=2, e=2),
+                in1=staged["gain", n].rearrange("m (p u e) -> m u p e", u=2, e=2),
+                op=MULT,
+            )
 
         def turn_y(n, tiles):
             bank = turn_bank("y_bank%d%d" % (n, tiles[0]))
@@ -300,83 +327,133 @@ def tile_displaced_overlap_table_k1_kernel(
 
         def quantize_y(n, tiles):
             cols = slice(tiles[0] * P, (tiles[-1] + 1) * P)
-            quantize((y_codes[n], y_scales[n]), cols, staged.pop(("y_grouped", n, tiles)))
+            quantize((y_codes[n], y_scales[:, n, :]), cols, staged.pop(("y_grouped", n, tiles)))
+
+        def store_codes(n, cols):
             words = out_1[n].rearrange("p m t -> p (m t)").bitcast(I32)
             nc.sync.dma_start(out=words[:, cols], in_=y_codes[n][:, cols].bitcast(I32))
-            if tiles[-1] == TILES - 1:
-                for q in range(4):
-                    queue = nc.scalar if n == NG - 1 and q % 2 == 1 else nc.sync
-                    queue.dma_start(
-                        out=out_2[n, 4 * q : 4 * q + 4, :].bitcast(I32),
-                        in_=y_scales[n][32 * q : 32 * q + 4, :].bitcast(I32),
-                    )
 
-        blocks = [(1, 0, 0), (1, 1, 0), (1, 0, 1), (1, 1, 1), (1, 2, 0), (1, 2, 1)]
+        def store_scales(groups, queues):
+            for q in range(4):
+                queues[q % len(queues)].dma_start(
+                    out=out_2[groups, 4 * q : 4 * q + 4, :].rearrange("n r m -> r n m").bitcast(I32),
+                    in_=y_scales[32 * q : 32 * q + 4, groups, :].bitcast(I32),
+                )
+
+        blocks = [(1, c, n) for n in range(KG) for c in range(CHUNKS)]
         blocks = blocks + [(2, c, n) for c in range(CHUNKS) for n in range(KG)]
-        units = [(n, i) for n in range(NG) for i in range(TILES)]
+        pairs = [(n, c) for n in range(NG) for c in range(CHUNKS)]
         fin_items = [(g, n, h) for n in range(NG) for g in range(KG) for h in range(2)]
 
         order_d(0)
         turn_x(0)
+        order_d(1)
         group_w("scalar", 0, 0, 1)
         group_w("vector", 0, 0, 0)
         turn_x(1)
-        order_d_scales()
+        quantize_w(0, 0, 1)
         quantize_w(0, 0, 0)
         group_w("scalar", 1, 0, 1)
-        quantize_w(0, 0, 1)
-        quantize_x(0)
         group_w("vector", 1, 0, 0)
+        quantize_x(0)
         turn_x(2)
         turn_x(3)
-        order_d(1)
         quantize_w(1, 0, 0)
         quantize_w(1, 0, 1)
         multiply_block(*blocks[0])
         group_w("scalar", 0, 1, 1)
         quantize_x(1)
-        group_w("vector", 0, 1, 0)
-        group_w("scalar", 1, 1, 1)
+        group_w("scalar", 0, 1, 0)
+        multiply_block(*blocks[1])
         turn_x(4)
         turn_x(5)
-        multiply_block(*blocks[1])
-        group_w("vector", 1, 1, 0)
-        quantize_w(0, 1, 0)
-        quantize_w(0, 1, 1)
-        quantize_w(1, 1, 0)
+        group_w("scalar", 1, 1, 1)
 
-        fin_at = {2: 0, 4: 1, 5: 2, 7: 3, 10: 4, 12: 5, 13: 6, 14: 7, 16: 8, 17: 9, 19: 10, 20: 11}
-        fin_on_vector = (1, 4, 8)
         nb = len(blocks)
-        turns = {TILES * n + i + 1: (n, (i, i + 1)) for n in range(NG) for i in range(0, TILES, 2)}
-        turns[len(units) - 2] = (NG - 1, (TILES - 2,))
-        turns[len(units) - 1] = (NG - 1, (TILES - 1,))
-        for s in range(nb + len(units) + 5):
-            if 2 <= s + 1 < nb:
-                multiply_block(*blocks[s + 1])
-            if s < nb:
-                add_diagonal(*blocks[s])
-                group_block(*blocks[s])
+        filler = nb // 2 - 1
+        quantize_steps = [s for s in range(3, len(fin_items) + 4) if s != filler]
+
+        def group_fin_at(step, engine):
+            if 1 <= step <= len(fin_items):
+                group_fin(engine, *fin_items[step - 1])
+
+        def quantize_fin_at(step):
+            if step in quantize_steps:
+                quantize_fin(*fin_items[quantize_steps.index(step)])
+
+        for s in range(nb):
+            add_diagonal(*blocks[s], range(3))
+            if s >= 2:
+                quantize_block(*blocks[s - 2])
+            add_diagonal(*blocks[s], range(3, 4))
             if s == 0:
-                quantize_w(1, 1, 1)
+                quantize_w(0, 1, 1)
+                order_d_scales()
             if s == 1:
                 quantize_x(2)
-            if s in fin_at:
-                group_fin("vector" if fin_at[s] in fin_on_vector else "scalar", *fin_items[fin_at[s]])
-            if s - 2 in fin_at:
-                quantize_fin(*fin_items[fin_at[s - 2]])
-            if 0 <= s - 2 < nb:
-                quantize_block(*blocks[s - 2])
-            u = s - nb
-            if u - 3 in turns:
-                turn_y(*turns[u - 3])
-            if 0 <= u + 2 < len(units):
-                multiply_unit(*units[u + 2])
-            if 0 <= u < len(units):
-                add_rest(*units[u])
-            if u - 5 in turns:
-                quantize_y(*turns[u - 5])
-            if u - 3 in turns:
-                group_y(*turns[u - 3])
-            if 0 <= u - 1 < len(units):
-                weigh(*units[u - 1])
+                group_w("vector", 1, 1, 0)
+                quantize_w(0, 1, 0)
+                quantize_w(1, 1, 1)
+                quantize_w(1, 1, 0)
+            quantize_fin_at(s)
+            if s == filler:
+                group_fin_at(s, "vector")
+            if 2 <= s + 1 < nb:
+                multiply_block(*blocks[s + 1])
+            group_block(*blocks[s], 2 <= s)
+            if s != filler:
+                group_fin_at(s, "scalar")
+            if s == nb - 4:
+                nc.scalar.copy(out=gain_f32[:], in_=gain_col[:])
+        multiply_unit(0, 0)
+        multiply_unit(0, 1)
+        spread_gain(0)
+
+        last = len(pairs) - 1
+        for k, (n, c) in enumerate(pairs):
+            first, second = 2 * c, 2 * c + 1
+            before = pairs[k - 1]
+            add_rest(n, first)
+            if k < 2:
+                quantize_block(*blocks[nb - 2 + k])
+            if k >= 3:
+                quantize_y(pairs[k - 3][0], (2 * pairs[k - 3][1], 2 * pairs[k - 3][1] + 1))
+                if pairs[k - 3][1] == CHUNKS - 1:
+                    store_codes(pairs[k - 3][0], slice(0, M))
+                if pairs[k - 3] == (0, CHUNKS - 1):
+                    store_scales(slice(0, 1), [nc.sync])
+            weigh("gpsimd", n, first)
+            if k < last:
+                multiply_unit(pairs[k + 1][0], 2 * pairs[k + 1][1])
+            if k >= 2:
+                turn_y(pairs[k - 2][0], (2 * pairs[k - 2][1], 2 * pairs[k - 2][1] + 1))
+            if k >= 1:
+                round_y(before[0], 2 * before[1])
+                weigh("vector", before[0], 2 * before[1] + 1)
+            if k >= 2:
+                group_y(pairs[k - 2][0], (2 * pairs[k - 2][1], 2 * pairs[k - 2][1] + 1))
+            if k >= 1:
+                round_y(before[0], 2 * before[1] + 1)
+            add_rest(n, second)
+            quantize_fin_at(nb + k)
+            if c == 1 and n + 1 < NG:
+                spread_gain(n + 1)
+            if k < last:
+                multiply_unit(pairs[k + 1][0], 2 * pairs[k + 1][1] + 1)
+            group_fin_at(nb + k, "scalar")
+
+        n = NG - 1
+        turn_y(n, (2, 3))
+        weigh_and_round(n, 5)
+        round_y(n, 4)
+        quantize_y(n, (0, 1))
+        group_y(n, (2, 3))
+        weigh("vector", n, 5)
+        store_y(n, 5)
+        turn_y(n, (4, 5))
+        quantize_y(n, (2, 3))
+        store_codes(n, slice(0, 2 * CHUNK))
+        group_y(n, (4, 5))
+        quantize_y(n, (4, 5))
+        store_codes(n, slice(2 * CHUNK, M))
+        store_scales(slice(1, NG), [nc.scalar, nc.sync])

@@ -25,7 +25,7 @@ CHUNK = 256
 CHUNKS = M // CHUNK
 TILES = M // P
 HALF = GROUP // 2
-GPSIMD_ROWS = 96
+GPSIMD_ROWS = 128
 
 
 def tile_displaced_overlap_table_k1_kernel(
@@ -45,7 +45,7 @@ def tile_displaced_overlap_table_k1_kernel(
             return kept(name + "_codes", [P, width], U32), kept(name + "_scales", [P, width], U8)
 
         def grouped_tile(name):
-            return ring.tile([P, 4 * CHUNK], BF16, name=name, tag="grouped", bufs=8, align_bytes=64)
+            return ring.tile([P, 4 * CHUNK], BF16, name=name, tag="grouped", bufs=4, align_bytes=64)
 
         def acc_bank(name):
             return psum.tile([P, GROUP], F32, name=name, tag="acc", bufs=4)
@@ -108,17 +108,17 @@ def tile_displaced_overlap_table_k1_kernel(
         load_x(0)
         load_d(1)
         load_rows(w_raw[0, 0], w, 0, 0)
+        for q in range(4):
+            nc.sync.dma_start(
+                out=ds_raw[32 * q : 32 * q + 4, :, :].bitcast(I32),
+                in_=d_scales[:, 4 * q : 4 * q + 4, :].rearrange("g r n -> r g n").bitcast(I32),
+            )
         load_x(1)
         load_rows(w_raw[1, 0], w, 1, 0)
         load_x(2)
         load_x(3)
         nc.sync.dma_start(out=wd[:], in_=w_diag.rearrange("(g p t) -> p g t", p=P, t=PACK))
         load_rows(w_raw[0, 1], w, 0, 1)
-        for q in range(4):
-            nc.sync.dma_start(
-                out=ds_raw[32 * q : 32 * q + 4, :, :].bitcast(I32),
-                in_=d_scales[:, 4 * q : 4 * q + 4, :].rearrange("g r n -> r g n").bitcast(I32),
-            )
         load_x(4)
         load_x(5)
         load_rows(w_raw[1, 1], w, 1, 1)
@@ -178,12 +178,15 @@ def tile_displaced_overlap_table_k1_kernel(
             )
 
         def group_fin(engine, g, n, h):
-            dst = grouped_tile("f_grouped%d%d%d" % (g, n, h))
+            if h == 0:
+                staged["f", g, n] = ring.tile(
+                    [P, PACK * GROUP], BF16, name="f_grouped%d%d" % (g, n), tag="fin", bufs=2, align_bytes=64
+                )
+            dst = staged["f", g, n][:, h * PACK * HALF : (h + 1) * PACK * HALF]
             interleave(engine, dst, f_raw[g, n][:, :, h * HALF : (h + 1) * HALF])
-            staged["f", g, n, h] = dst
 
-        def quantize_fin(g, n, h):
-            quantize(f_mx[g, n], slice(h * HALF, (h + 1) * HALF), staged.pop(("f", g, n, h)))
+        def quantize_fin(g, n):
+            quantize(f_mx[g, n], slice(0, GROUP), staged.pop(("f", g, n)))
 
         def multiply_block(stage, c, n):
             banks = []
@@ -240,7 +243,7 @@ def tile_displaced_overlap_table_k1_kernel(
             staged["slots", stage, c, n] = dst
 
         def group_block(stage, c, n, shared):
-            dst = grouped_tile("x_grouped%d_%d%d" % (stage, c, n))
+            dst = ring.tile([P, PACK * CHUNK], BF16, name="x_grouped%d_%d%d" % (stage, c, n), tag="block", align_bytes=64)
             src = staged.pop(("slots", stage, c, n))
             rows = GPSIMD_ROWS if shared else 0
             if shared:
@@ -351,6 +354,7 @@ def tile_displaced_overlap_table_k1_kernel(
         group_w("scalar", 0, 0, 1)
         group_w("vector", 0, 0, 0)
         turn_x(1)
+        order_d_scales()
         quantize_w(0, 0, 1)
         quantize_w(0, 0, 0)
         group_w("scalar", 1, 0, 1)
@@ -362,47 +366,44 @@ def tile_displaced_overlap_table_k1_kernel(
         quantize_w(1, 0, 1)
         multiply_block(*blocks[0])
         group_w("scalar", 0, 1, 1)
+        group_w("vector", 0, 1, 0)
         quantize_x(1)
-        group_w("scalar", 0, 1, 0)
-        multiply_block(*blocks[1])
         turn_x(4)
         turn_x(5)
+        multiply_block(*blocks[1])
         group_w("scalar", 1, 1, 1)
 
         nb = len(blocks)
         filler = nb // 2 - 1
-        quantize_steps = [s for s in range(3, len(fin_items) + 4) if s != filler]
-
-        def group_fin_at(step, engine):
-            if 1 <= step <= len(fin_items):
-                group_fin(engine, *fin_items[step - 1])
+        fin_quantize_at = [4, 6, 7, 9, 11, 14]
 
         def quantize_fin_at(step):
-            if step in quantize_steps:
-                quantize_fin(*fin_items[quantize_steps.index(step)])
+            if step in fin_quantize_at:
+                quantize_fin(*fin_items[2 * fin_quantize_at.index(step)][:2])
 
         for s in range(nb):
             add_diagonal(*blocks[s], range(3))
-            if s >= 2:
+            if s == filler:
                 quantize_block(*blocks[s - 2])
             add_diagonal(*blocks[s], range(3, 4))
             if s == 0:
                 quantize_w(0, 1, 1)
-                order_d_scales()
+                quantize_w(0, 1, 0)
             if s == 1:
                 quantize_x(2)
                 group_w("vector", 1, 1, 0)
-                quantize_w(0, 1, 0)
                 quantize_w(1, 1, 1)
                 quantize_w(1, 1, 0)
             quantize_fin_at(s)
             if s == filler:
-                group_fin_at(s, "vector")
+                group_fin("vector", *fin_items[s - 1])
+            elif s >= 2:
+                quantize_block(*blocks[s - 2])
             if 2 <= s + 1 < nb:
                 multiply_block(*blocks[s + 1])
-            group_block(*blocks[s], 2 <= s)
-            if s != filler:
-                group_fin_at(s, "scalar")
+            group_block(*blocks[s], 2 <= s < nb - 1)
+            if s >= 1:
+                group_fin("scalar", *fin_items[s - 1 if s < filler else s])
             if s == nb - 4:
                 nc.scalar.copy(out=gain_f32[:], in_=gain_col[:])
         multiply_unit(0, 0)
@@ -416,6 +417,7 @@ def tile_displaced_overlap_table_k1_kernel(
             add_rest(n, first)
             if k < 2:
                 quantize_block(*blocks[nb - 2 + k])
+            quantize_fin_at(nb + k)
             if k >= 3:
                 quantize_y(pairs[k - 3][0], (2 * pairs[k - 3][1], 2 * pairs[k - 3][1] + 1))
                 if pairs[k - 3][1] == CHUNKS - 1:
@@ -435,12 +437,10 @@ def tile_displaced_overlap_table_k1_kernel(
             if k >= 1:
                 round_y(before[0], 2 * before[1] + 1)
             add_rest(n, second)
-            quantize_fin_at(nb + k)
             if c == 1 and n + 1 < NG:
                 spread_gain(n + 1)
             if k < last:
                 multiply_unit(pairs[k + 1][0], 2 * pairs[k + 1][1] + 1)
-            group_fin_at(nb + k, "scalar")
 
         n = NG - 1
         turn_y(n, (2, 3))

@@ -45,7 +45,7 @@ def tile_displaced_overlap_table_k1_kernel(
             return kept(name + "_codes", [P, width], U32), kept(name + "_scales", [P, width], U8)
 
         def grouped_tile(name):
-            return ring.tile([P, 4 * CHUNK], BF16, name=name, tag="grouped", bufs=4, align_bytes=64)
+            return ring.tile([P, 4 * CHUNK], BF16, name=name, tag="grouped", bufs=5, align_bytes=64)
 
         def acc_bank(name):
             return psum.tile([P, GROUP], F32, name=name, tag="acc", bufs=4)
@@ -56,8 +56,6 @@ def tile_displaced_overlap_table_k1_kernel(
         def copy_on(engine, out, in_):
             if engine == "vector":
                 nc.vector.tensor_copy(out=out, in_=in_)
-            elif engine == "gpsimd":
-                nc.gpsimd.tensor_scalar(out=out, in0=in_, scalar1=1.0, scalar2=0.0, op0=MULT, op1=ADD)
             else:
                 nc.scalar.copy(out=out, in_=in_)
 
@@ -69,9 +67,9 @@ def tile_displaced_overlap_table_k1_kernel(
         w_raw = {(g, n): kept("w_raw%d%d" % (g, n), [P, PACK, GROUP], BF16) for g in range(KG) for n in range(KG)}
         f_raw = {(g, n): kept("f_raw%d%d" % (g, n), [P, PACK, GROUP], BF16) for g in range(KG) for n in range(NG)}
         d_raw = [kept("d_raw%d" % g, [P, 2 * K], U8) for g in range(KG)]
-        ds_raw = kept("ds_raw", [P, KG, K], U8)
+        ds_raw = kept("ds_raw", [P, K], U8)
         d_codes = [kept("d_codes%d" % g, [P, 2 * K], U8) for g in range(KG)]
-        ds = kept("ds", [P, KG * K], U8)
+        ds = [kept("ds%d" % g, [P, K], U8) for g in range(KG)]
         wd = kept("wd", [P, KG, PACK], BF16)
         dd = kept("dd", [P, KG, PACK], BF16)
         rest_sb = [kept("rest%d" % n, [P, TILES, GROUP], BF16) for n in range(NG)]
@@ -103,34 +101,30 @@ def tile_displaced_overlap_table_k1_kernel(
             nc.sync.dma_start(out=rest_sb[n][:], in_=cols.rearrange("(i p) c -> p i c", p=P))
 
         make_identity(nc, ident[:])
-        nc.vector.memset(ds_raw[:].rearrange("p g n -> p (g n)").bitcast(I32), 0)
+        nc.vector.memset(ds_raw[:].bitcast(I32), 0)
+        nc.vector.memset(ds[1][:].bitcast(I32), 0)
         load_d(0)
         load_x(0)
         load_d(1)
         load_rows(w_raw[0, 0], w, 0, 0)
-        for q in range(4):
-            nc.sync.dma_start(
-                out=ds_raw[32 * q : 32 * q + 4, :, :].bitcast(I32),
-                in_=d_scales[:, 4 * q : 4 * q + 4, :].rearrange("g r n -> r g n").bitcast(I32),
-            )
         load_x(1)
         load_rows(w_raw[1, 0], w, 1, 0)
         load_x(2)
         load_x(3)
         nc.sync.dma_start(out=wd[:], in_=w_diag.rearrange("(g p t) -> p g t", p=P, t=PACK))
         load_rows(w_raw[0, 1], w, 0, 1)
+        for q in range(4):
+            nc.sync.dma_start(
+                out=ds_raw[32 * q : 32 * q + 4 * KG, :].bitcast(I32),
+                in_=d_scales[:, 4 * q : 4 * q + 4, :].bitcast(I32),
+            )
         load_x(4)
         load_x(5)
         load_rows(w_raw[1, 1], w, 1, 1)
         nc.sync.dma_start(out=dd[:], in_=d_diag.rearrange("(g p t) -> p g t", p=P, t=PACK))
-        for n in range(NG):
+        for n in range(NG - 1):
             for g in range(KG):
                 load_rows(f_raw[g, n], fin, g, n)
-        nc.sync.dma_start(out=gain_col[:], in_=gain.rearrange("(n p t) -> p n t", p=P, t=PACK))
-        load_rest(0)
-        nc.sync.dma_start(out=gain_sb[:], in_=gain.partition_broadcast(P))
-        load_rest(1)
-        load_rest(2)
 
         staged = {}
 
@@ -142,9 +136,20 @@ def tile_displaced_overlap_table_k1_kernel(
 
         def order_d_scales():
             nc.vector.tensor_copy(
-                out=ds[:].rearrange("p (h t m) -> p h t m", t=PACK, m=P),
-                in_=ds_raw[:].rearrange("p g (n m t) -> p (g n) t m", t=PACK, m=P),
+                out=ds[0][:].rearrange("p (n t m) -> p n t m", t=PACK, m=P),
+                in_=ds_raw[:].rearrange("p (n m t) -> p n t m", t=PACK, m=P),
             )
+            for q in range(4):
+                nc.sync.dma_start(
+                    out=ds[1][32 * q : 32 * q + 4, :].bitcast(I32), in_=ds[0][32 * q + 4 : 32 * q + 8, :].bitcast(I32)
+                )
+            for g in range(KG):
+                load_rows(f_raw[g, NG - 1], fin, g, NG - 1)
+            nc.sync.dma_start(out=gain_col[:], in_=gain.rearrange("(n p t) -> p n t", p=P, t=PACK))
+            load_rest(0)
+            nc.sync.dma_start(out=gain_sb[:], in_=gain.partition_broadcast(P))
+            load_rest(1)
+            load_rest(2)
 
         def turn_x(i):
             words = x_raw[i][:].bitcast(F32)
@@ -214,7 +219,7 @@ def tile_displaced_overlap_table_k1_kernel(
                                 nc.tensor.matmul_mx(
                                     out=bank[:, e * CHUNK + a * P : e * CHUNK + (a + 1) * P],
                                     lhsT=d_codes[g][:, 2 * col0 : 2 * (col0 + P)].bitcast(FP4X4),
-                                    lhsT_scale=ds[:, g * K + col0 : g * K + col0 + P],
+                                    lhsT_scale=ds[g][:, col0 : col0 + P],
                                     rhs=x1_mx[c, g][0][:, a * P : (a + 1) * P].bitcast(FP8X4),
                                     rhs_scale=x1_mx[c, g][1][:, a * P : (a + 1) * P],
                                     start=(g == 0),
@@ -247,7 +252,14 @@ def tile_displaced_overlap_table_k1_kernel(
             src = staged.pop(("slots", stage, c, n))
             rows = GPSIMD_ROWS if shared else 0
             if shared:
-                interleave("gpsimd", dst[:, : PACK * rows], src[:, :, :rows])
+                nc.gpsimd.tensor_scalar(
+                    out=dst[:, : PACK * rows].rearrange("p (m t) -> p m t", t=PACK),
+                    in0=src[:, :, :rows].rearrange("p t m -> p m t"),
+                    scalar1=1.0,
+                    scalar2=0.0,
+                    op0=MULT,
+                    op1=ADD,
+                )
             interleave("scalar", dst[:, PACK * rows :], src[:, :, rows:])
             staged["grouped", stage, c, n] = dst
 
@@ -354,7 +366,6 @@ def tile_displaced_overlap_table_k1_kernel(
         group_w("scalar", 0, 0, 1)
         group_w("vector", 0, 0, 0)
         turn_x(1)
-        order_d_scales()
         quantize_w(0, 0, 1)
         quantize_w(0, 0, 0)
         group_w("scalar", 1, 0, 1)
@@ -374,36 +385,40 @@ def tile_displaced_overlap_table_k1_kernel(
         group_w("scalar", 1, 1, 1)
 
         nb = len(blocks)
-        filler = nb // 2 - 1
-        fin_quantize_at = [4, 6, 7, 9, 11, 14]
+        fin_group_at = dict(zip([1] + list(range(3, nb + 1)), list(range(10)) + [11]))
+        fin_quantize_at = [5, 7, 9, 11, nb + 2, nb + 3]
+        quantize_at = {s: [s - 2] for s in range(2, nb)}
+        quantize_at[4] = [3, 2]
+        quantize_at[5] = []
+
+        def group_fin_at(step):
+            if step in fin_group_at:
+                group_fin("scalar", *fin_items[fin_group_at[step]])
 
         def quantize_fin_at(step):
             if step in fin_quantize_at:
                 quantize_fin(*fin_items[2 * fin_quantize_at.index(step)][:2])
 
         for s in range(nb):
-            add_diagonal(*blocks[s], range(3))
-            if s == filler:
-                quantize_block(*blocks[s - 2])
-            add_diagonal(*blocks[s], range(3, 4))
+            add_diagonal(*blocks[s], range(PACK))
             if s == 0:
                 quantize_w(0, 1, 1)
                 quantize_w(0, 1, 0)
+                order_d_scales()
             if s == 1:
                 quantize_x(2)
                 group_w("vector", 1, 1, 0)
                 quantize_w(1, 1, 1)
                 quantize_w(1, 1, 0)
             quantize_fin_at(s)
-            if s == filler:
-                group_fin("vector", *fin_items[s - 1])
-            elif s >= 2:
-                quantize_block(*blocks[s - 2])
+            for b in quantize_at.get(s, ()):
+                quantize_block(*blocks[b])
+            if s == nb - 1:
+                group_fin("vector", *fin_items[10])
             if 2 <= s + 1 < nb:
                 multiply_block(*blocks[s + 1])
             group_block(*blocks[s], 2 <= s < nb - 1)
-            if s >= 1:
-                group_fin("scalar", *fin_items[s - 1 if s < filler else s])
+            group_fin_at(s)
             if s == nb - 4:
                 nc.scalar.copy(out=gain_f32[:], in_=gain_col[:])
         multiply_unit(0, 0)
@@ -418,11 +433,11 @@ def tile_displaced_overlap_table_k1_kernel(
             if k < 2:
                 quantize_block(*blocks[nb - 2 + k])
             quantize_fin_at(nb + k)
-            if k >= 3:
-                quantize_y(pairs[k - 3][0], (2 * pairs[k - 3][1], 2 * pairs[k - 3][1] + 1))
-                if pairs[k - 3][1] == CHUNKS - 1:
-                    store_codes(pairs[k - 3][0], slice(0, M))
-                if pairs[k - 3] == (0, CHUNKS - 1):
+            if k >= 4:
+                quantize_y(pairs[k - 4][0], (2 * pairs[k - 4][1], 2 * pairs[k - 4][1] + 1))
+                if pairs[k - 4][1] == CHUNKS - 1:
+                    store_codes(pairs[k - 4][0], slice(0, M))
+                if pairs[k - 4] == (0, CHUNKS - 1):
                     store_scales(slice(0, 1), [nc.sync])
             weigh("gpsimd", n, first)
             if k < last:
@@ -432,20 +447,23 @@ def tile_displaced_overlap_table_k1_kernel(
             if k >= 1:
                 round_y(before[0], 2 * before[1])
                 weigh("vector", before[0], 2 * before[1] + 1)
-            if k >= 2:
-                group_y(pairs[k - 2][0], (2 * pairs[k - 2][1], 2 * pairs[k - 2][1] + 1))
             if k >= 1:
                 round_y(before[0], 2 * before[1] + 1)
+            if k >= 2:
+                group_y(pairs[k - 2][0], (2 * pairs[k - 2][1], 2 * pairs[k - 2][1] + 1))
             add_rest(n, second)
             if c == 1 and n + 1 < NG:
                 spread_gain(n + 1)
             if k < last:
                 multiply_unit(pairs[k + 1][0], 2 * pairs[k + 1][1] + 1)
+            group_fin_at(nb + k)
 
         n = NG - 1
         turn_y(n, (2, 3))
         weigh_and_round(n, 5)
         round_y(n, 4)
+        quantize_y(n - 1, (4, 5))
+        store_codes(n - 1, slice(0, M))
         quantize_y(n, (0, 1))
         group_y(n, (2, 3))
         weigh("vector", n, 5)

from contextlib import ExitStack

import concourse.mybir as mybir
from concourse.masks import make_identity

M, K, N = 768, 1024, 1536
FLOPS = 2 * M * K * (K + K + N)

F32 = mybir.dt.float32
BF16 = mybir.dt.bfloat16
U32 = mybir.dt.uint32
I32 = mybir.dt.int32
U8 = mybir.dt.uint8
FP8X4 = mybir.dt.float8_e4m3fn_x4
FP4X4 = mybir.dt.float4_e2m1fn_x4
ADD = mybir.AluOpType.add
MULT = mybir.AluOpType.mult

P = 128
PACK = 4
GROUP = P * PACK
KG = K // GROUP
NG = N // GROUP
CHUNK = 256
CHUNKS = M // CHUNK
TILES = M // P
HALF = GROUP // 2
GPSIMD_ROWS = 128


def tile_displaced_overlap_table_k1_kernel(
    tc, x, w, w_diag, d_words, d_scales, d_diag, fin, rest, gain, out_0, out_1, out_2
):
    nc = tc.nc
    with ExitStack() as ctx:
        keep = ctx.enter_context(tc.tile_pool(name="keep", bufs=1))
        ring = ctx.enter_context(tc.tile_pool(name="ring", bufs=2))
        psum = ctx.enter_context(tc.psum_pool(name="psum", bufs=1))
        ctx.enter_context(tc.manual_schedule())

        def kept(name, shape, dtype):
            return keep.tile(shape, dtype, name=name, align_bytes=64)

        def mx_tiles(name, width):
            return kept(name + "_codes", [P, width], U32), kept(name + "_scales", [P, width], U8)

        def grouped_tile(name):
            return ring.tile([P, 4 * CHUNK], BF16, name=name, tag="grouped", bufs=5, align_bytes=64)

        def acc_bank(name):
            return psum.tile([P, GROUP], F32, name=name, tag="acc", bufs=4)

        def turn_bank(name):
            return psum.tile([P, 4, P], F32, name=name, tag="turn", bufs=2)

        def copy_on(engine, out, in_):
            if engine == "vector":
                nc.vector.tensor_copy(out=out, in_=in_)
            else:
                nc.scalar.copy(out=out, in_=in_)

        def quantize(mx, cols, src):
            nc.vector.quantize_mx(out=mx[0][:, cols].bitcast(FP8X4), scales=mx[1][:, cols], in_=src[:])

        ident = kept("ident", [P, P], F32)
        x_raw = [kept("x_raw%d" % i, [P, K], BF16) for i in range(TILES)]
        w_raw = {(g, n): kept("w_raw%d%d" % (g, n), [P, PACK, GROUP], BF16) for g in range(KG) for n in range(KG)}
        f_raw = {(g, n): kept("f_raw%d%d" % (g, n), [P, PACK, GROUP], BF16) for g in range(KG) for n in range(NG)}
        d_raw = [kept("d_raw%d" % g, [P, 2 * K], U8) for g in range(KG)]
        ds_raw = kept("ds_raw", [P, K], U8)
        d_codes = [kept("d_codes%d" % g, [P, 2 * K], U8) for g in range(KG)]
        ds = [kept("ds%d" % g, [P, K], U8) for g in range(KG)]
        wd = kept("wd", [P, KG, PACK], BF16)
        dd = kept("dd", [P, KG, PACK], BF16)
        rest_sb = [kept("rest%d" % n, [P, TILES, GROUP], BF16) for n in range(NG)]
        gain_sb = kept("gain_sb", [P, N], BF16)
        gain_col = kept("gain_col", [P, NG, PACK], BF16)
        gain_f32 = kept("gain_f32", [P, NG, PACK], F32)
        x_t = [kept("x_t%d" % c, [P, KG, CHUNK, PACK], BF16) for c in range(CHUNKS)]
        x_mx = [mx_tiles("x%d" % c, KG * CHUNK) for c in range(CHUNKS)]
        w_mx = {key: mx_tiles("w%d%d" % key, GROUP) for key in w_raw}
        f_mx = {key: mx_tiles("f%d%d" % key, GROUP) for key in f_raw}
        x1 = {(c, g): kept("x1_%d%d" % (c, g), [P, PACK, CHUNK], F32) for c in range(CHUNKS) for g in range(KG)}
        x1_mx = {key: mx_tiles("x1_%d%d" % key, CHUNK) for key in x1}
        x2_mx = {key: mx_tiles("x2_%d%d" % key, CHUNK) for key in x1}
        y_codes = [kept("y_codes%d" % n, [P, M], U32) for n in range(NG)]
        y_scales = kept("y_scales", [P, NG, M], U8)

        def load_rows(dst, src, g, n):
            rows = src[g * GROUP : (g + 1) * GROUP, n * GROUP : (n + 1) * GROUP]
            nc.sync.dma_start(out=dst[:], in_=rows.rearrange("(p j) c -> p j c", j=PACK))

        def load_x(i):
            nc.sync.dma_start(out=x_raw[i][:], in_=x[i * P : (i + 1) * P, :])

        def load_d(g):
            nc.sync.dma_start(out=d_raw[g][:].bitcast(I32), in_=d_words[g].bitcast(I32))

        def load_rest(n):
            cols = rest[:, n * GROUP : (n + 1) * GROUP]
            nc.sync.dma_start(out=rest_sb[n][:], in_=cols.rearrange("(i p) c -> p i c", p=P))

        make_identity(nc, ident[:])
        nc.vector.memset(ds_raw[:].bitcast(I32), 0)
        nc.vector.memset(ds[1][:].bitcast(I32), 0)
        load_d(0)
        load_x(0)
        load_d(1)
        load_rows(w_raw[0, 0], w, 0, 0)
        load_x(1)
        load_rows(w_raw[1, 0], w, 1, 0)
        load_x(2)
        load_x(3)
        nc.sync.dma_start(out=wd[:], in_=w_diag.rearrange("(g p t) -> p g t", p=P, t=PACK))
        load_rows(w_raw[0, 1], w, 0, 1)
        for q in range(4):
            nc.sync.dma_start(
                out=ds_raw[32 * q : 32 * q + 4 * KG, :].bitcast(I32),
                in_=d_scales[:, 4 * q : 4 * q + 4, :].bitcast(I32),
            )
        load_x(4)
        load_x(5)
        load_rows(w_raw[1, 1], w, 1, 1)
        nc.sync.dma_start(out=dd[:], in_=d_diag.rearrange("(g p t) -> p g t", p=P, t=PACK))
        for n in range(NG - 1):
            for g in range(KG):
                load_rows(f_raw[g, n], fin, g, n)

        staged = {}

        def order_d(g):
            nc.vector.tensor_copy(
                out=d_codes[g][:].rearrange("p (n t m b) -> p n t m b", n=KG, t=PACK, b=2),
                in_=d_raw[g][:].rearrange("p (n m t b) -> p n t m b", n=KG, t=PACK, b=2),
            )

        def order_d_scales():
            nc.vector.tensor_copy(
                out=ds[0][:].rearrange("p (n t m) -> p n t m", t=PACK, m=P),
                in_=ds_raw[:].rearrange("p (n m t) -> p n t m", t=PACK, m=P),
            )
            for q in range(4):
                nc.sync.dma_start(
                    out=ds[1][32 * q : 32 * q + 4, :].bitcast(I32), in_=ds[0][32 * q + 4 : 32 * q + 8, :].bitcast(I32)
                )
            for g in range(KG):
                load_rows(f_raw[g, NG - 1], fin, g, NG - 1)
            nc.sync.dma_start(out=gain_col[:], in_=gain.rearrange("(n p t) -> p n t", p=P, t=PACK))
            load_rest(0)
            nc.sync.dma_start(out=gain_sb[:], in_=gain.partition_broadcast(P))
            load_rest(1)
            load_rest(2)

        def turn_x(i):
            words = x_raw[i][:].bitcast(F32)
            bank = turn_bank("x_bank%d" % i)
            for g in range(KG):
                for u in range(2):
                    nc.tensor.transpose(bank[:, 2 * g + u, :], words[:, HALF * g + u : HALF * (g + 1) : 2], ident[:])
            c, a = divmod(i, 2)
            dst = x_t[c][:].rearrange("p g m t -> p (g m t)").bitcast(F32).rearrange("p (g m u) -> p g m u", g=KG, u=2)
            nc.scalar.copy(out=dst[:, :, a * P : (a + 1) * P, :], in_=bank[:].rearrange("p (g u) m -> p g m u", u=2))

        def quantize_x(c):
            nc.vector.quantize_mx(
                out=x_mx[c][0][:].bitcast(FP8X4), scales=x_mx[c][1][:], in_=x_t[c][:].rearrange("p g m t -> p (g m t)")
            )

        def group_w(engine, g, n, h):
            dst = grouped_tile("w_grouped%d%d%d" % (g, n, h))
            src = w_raw[g, n][:].rearrange("p j (m t) -> p m j t", t=PACK)[:, :, :, 2 * h : 2 * h + 2]
            copy_on(engine, dst[:].rearrange("p (t m j) -> p m j t", t=2, j=PACK), src)
            staged["w", g, n, h] = dst

        def quantize_w(g, n, h):
            quantize(w_mx[g, n], slice(h * HALF, (h + 1) * HALF), staged.pop(("w", g, n, h)))

        def interleave(engine, dst, src):
            copy_on(
                engine,
                dst[:].rearrange("p (c i t) -> p c t i", i=4, t=PACK),
                src.rearrange("p t (c i) -> p c t i", i=4),
            )

        def group_fin(engine, g, n, h):
            if h == 0:
                staged["f", g, n] = ring.tile(
                    [P, PACK * GROUP], BF16, name="f_grouped%d%d" % (g, n), tag="fin", bufs=2, align_bytes=64
                )
            dst = staged["f", g, n][:, h * PACK * HALF : (h + 1) * PACK * HALF]
            interleave(engine, dst, f_raw[g, n][:, :, h * HALF : (h + 1) * HALF])

        def quantize_fin(g, n):
            quantize(f_mx[g, n], slice(0, GROUP), staged.pop(("f", g, n)))

        def multiply_block(stage, c, n):
            banks = []
            for pair in range(2):
                bank = acc_bank("acc%d_%d%d%d" % (stage, c, n, pair))
                banks.append(bank)
                for e in range(2):
                    t = 2 * pair + e
                    if stage == 1:
                        for g in range(KG):
                            cols = slice(g * CHUNK, (g + 1) * CHUNK)
                            nc.tensor.matmul_mx(
                                out=bank[:, e * CHUNK : (e + 1) * CHUNK],
                                lhsT=w_mx[g, n][0][:, t * P : (t + 1) * P].bitcast(FP8X4),
                                lhsT_scale=w_mx[g, n][1][:, t * P : (t + 1) * P],
                                rhs=x_mx[c][0][:, cols].bitcast(FP8X4),
                                rhs_scale=x_mx[c][1][:, cols],
                                start=(g == 0),
                                stop=(g == KG - 1),
                            )
                    else:
                        col0 = n * GROUP + t * P
                        for a in range(2):
                            for g in range(KG):
                                nc.tensor.matmul_mx(
                                    out=bank[:, e * CHUNK + a * P : e * CHUNK + (a + 1) * P],
                                    lhsT=d_codes[g][:, 2 * col0 : 2 * (col0 + P)].bitcast(FP4X4),
                                    lhsT_scale=ds[g][:, col0 : col0 + P],
                                    rhs=x1_mx[c, g][0][:, a * P : (a + 1) * P].bitcast(FP8X4),
                                    rhs_scale=x1_mx[c, g][1][:, a * P : (a + 1) * P],
                                    start=(g == 0),
                                    stop=(g == KG - 1),
                                )
            staged["acc", stage, c, n] = banks

        def add_diagonal(stage, c, n, slots):
            banks = staged["acc", stage, c, n]
            if stage == 1:
                dst = x1[c, n]
            elif slots[0] == 0:
                dst = ring.tile([P, PACK, CHUNK], BF16, name="x2_%d%d" % (c, n), tag="x2", bufs=3)
            else:
                dst = staged["slots", stage, c, n]
            for t in slots:
                pair, e = divmod(t, 2)
                nc.vector.scalar_tensor_tensor(
                    out=dst[:, t, :],
                    in0=x_t[c][:, n, :, t] if stage == 1 else x1[c, n][:, t, :],
                    scalar=(wd if stage == 1 else dd)[:, n, t : t + 1],
                    in1=banks[pair][:, e * CHUNK : (e + 1) * CHUNK],
                    op0=MULT,
                    op1=ADD,
                )
            staged["slots", stage, c, n] = dst

        def group_block(stage, c, n, shared):
            dst = ring.tile([P, PACK * CHUNK], BF16, name="x_grouped%d_%d%d" % (stage, c, n), tag="block", align_bytes=64)
            src = staged.pop(("slots", stage, c, n))
            rows = GPSIMD_ROWS if shared else 0
            if shared:
                nc.gpsimd.tensor_scalar(
                    out=dst[:, : PACK * rows].rearrange("p (m t) -> p m t", t=PACK),
                    in0=src[:, :, :rows].rearrange("p t m -> p m t"),
                    scalar1=1.0,
                    scalar2=0.0,
                    op0=MULT,
                    op1=ADD,
                )
            interleave("scalar", dst[:, PACK * rows :], src[:, :, rows:])
            staged["grouped", stage, c, n] = dst

        def quantize_block(stage, c, n):
            mx = x1_mx if stage == 1 else x2_mx
            quantize(mx[c, n], slice(0, CHUNK), staged.pop(("grouped", stage, c, n)))

        def multiply_unit(n, i):
            bank = acc_bank("acc3_%d%d" % (n, i))
            c, a = divmod(i, 2)
            for g in range(KG):
                nc.tensor.matmul_mx(
                    out=bank[:],
                    lhsT=x2_mx[c, g][0][:, a * P : (a + 1) * P].bitcast(FP8X4),
                    lhsT_scale=x2_mx[c, g][1][:, a * P : (a + 1) * P],
                    rhs=f_mx[g, n][0][:].bitcast(FP8X4),
                    rhs_scale=f_mx[g, n][1][:],
                    start=(g == 0),
                    stop=(g == KG - 1),
                )
            staged["acc3", n, i] = bank

        def add_rest(n, i):
            y = ring.tile([P, GROUP], F32, name="y%d%d" % (n, i), tag="y", bufs=10)
            nc.vector.tensor_tensor(out=y[:], in0=staged.pop(("acc3", n, i))[:], in1=rest_sb[n][:, i, :], op=ADD)
            staged["y", n, i] = y

        def spread_gain(n):
            bank = psum.tile([P, P, PACK], F32, name="gain_bank%d" % n, tag="gain", bufs=2)
            for t in range(PACK):
                nc.tensor.transpose(bank[:, :, t], gain_f32[:, n, t : t + 1].to_broadcast([P, P]), ident[:])
            staged["gain", n] = bank[:].rearrange("m p t -> m (p t)")

        def weigh(engine, n, i):
            y = staged["y", n, i]
            cols = slice(n * GROUP, (n + 1) * GROUP)
            if engine == "gpsimd":
                nc.gpsimd.tensor_tensor(out=y[:], in0=y[:], in1=gain_sb[:, cols], op=MULT)
            else:
                nc.vector.tensor_tensor(out=y[:], in0=y[:], in1=staged["gain", n], op=MULT)

        def store_y(n, i):
            rows = out_0[i * P : (i + 1) * P, n * GROUP : (n + 1) * GROUP]
            nc.sync.dma_start(out=rows, in_=staged.pop(("y", n, i))[:])

        def sorted_pairs(n, i):
            y_bf = ring.tile([P, GROUP], BF16, name="y_bf%d%d" % (n, i), tag="y_bf", bufs=6)
            staged["y_bf", n, i] = y_bf
            return y_bf[:].rearrange("m (u p e) -> m u p e", u=2, e=2)

        def round_y(n, i):
            y = staged["y", n, i]
            nc.scalar.copy(out=sorted_pairs(n, i), in_=y[:].rearrange("m (p u e) -> m u p e", u=2, e=2))
            store_y(n, i)

        def weigh_and_round(n, i):
            nc.vector.tensor_tensor(
                out=sorted_pairs(n, i),
                in0=staged["y", n, i][:].rearrange("m (p u e) -> m u p e", u=2, e=2),
                in1=staged["gain", n].rearrange("m (p u e) -> m u p e", u=2, e=2),
                op=MULT,
            )

        def turn_y(n, tiles):
            bank = turn_bank("y_bank%d%d" % (n, tiles[0]))
            for a, i in enumerate(tiles):
                words = staged.pop(("y_bf", n, i))[:].bitcast(F32)
                for u in range(2):
                    nc.tensor.transpose(bank[:, 2 * a + u, :], words[:, u * P : (u + 1) * P], ident[:])
            staged["y_bank", n, tiles] = bank

        def group_y(n, tiles):
            dst = grouped_tile("y_grouped%d%d" % (n, tiles[0]))
            width = len(tiles) * GROUP
            nc.scalar.copy(
                out=dst[:, :width].bitcast(F32).rearrange("p (a m u) -> p a m u", m=P, u=2),
                in_=staged.pop(("y_bank", n, tiles))[:, : 2 * len(tiles), :].rearrange("p (a u) m -> p a m u", u=2),
            )
            staged["y_grouped", n, tiles] = dst[:, :width]

        def quantize_y(n, tiles):
            cols = slice(tiles[0] * P, (tiles[-1] + 1) * P)
            quantize((y_codes[n], y_scales[:, n, :]), cols, staged.pop(("y_grouped", n, tiles)))

        def store_codes(n, cols):
            words = out_1[n].rearrange("p m t -> p (m t)").bitcast(I32)
            nc.sync.dma_start(out=words[:, cols], in_=y_codes[n][:, cols].bitcast(I32))

        def store_scales(groups, queues):
            for q in range(4):
                queues[q % len(queues)].dma_start(
                    out=out_2[groups, 4 * q : 4 * q + 4, :].rearrange("n r m -> r n m").bitcast(I32),
                    in_=y_scales[32 * q : 32 * q + 4, groups, :].bitcast(I32),
                )

        blocks = [(1, c, n) for n in range(KG) for c in range(CHUNKS)]
        blocks = blocks + [(2, c, n) for c in range(CHUNKS) for n in range(KG)]
        pairs = [(n, c) for n in range(NG) for c in range(CHUNKS)]
        fin_items = [(g, n, h) for n in range(NG) for g in range(KG) for h in range(2)]

        order_d(0)
        turn_x(0)
        order_d(1)
        group_w("scalar", 0, 0, 1)
        group_w("vector", 0, 0, 0)
        turn_x(1)
        quantize_w(0, 0, 1)
        quantize_w(0, 0, 0)
        group_w("scalar", 1, 0, 1)
        group_w("vector", 1, 0, 0)
        quantize_x(0)
        turn_x(2)
        turn_x(3)
        quantize_w(1, 0, 0)
        quantize_w(1, 0, 1)
        multiply_block(*blocks[0])
        group_w("scalar", 0, 1, 1)
        group_w("vector", 0, 1, 0)
        quantize_x(1)
        turn_x(4)
        turn_x(5)
        multiply_block(*blocks[1])
        group_w("scalar", 1, 1, 1)

        nb = len(blocks)
        fin_group_at = dict(zip([1] + list(range(3, nb + 1)), list(range(10)) + [11]))
        fin_quantize_at = [5, 7, 9, 11, nb + 2, nb + 3]
        quantize_at = {s: [s - 2] for s in range(2, nb)}
        quantize_at[4] = [3, 2]
        quantize_at[5] = []

        def group_fin_at(step):
            if step in fin_group_at:
                group_fin("scalar", *fin_items[fin_group_at[step]])

        def quantize_fin_at(step):
            if step in fin_quantize_at:
                quantize_fin(*fin_items[2 * fin_quantize_at.index(step)][:2])

        for s in range(nb):
            add_diagonal(*blocks[s], range(PACK))
            if s == 0:
                quantize_w(0, 1, 1)
                quantize_w(0, 1, 0)
                order_d_scales()
            if s == 1:
                quantize_x(2)
                group_w("vector", 1, 1, 0)
                quantize_w(1, 1, 1)
                quantize_w(1, 1, 0)
            quantize_fin_at(s)
            for b in quantize_at.get(s, ()):
                quantize_block(*blocks[b])
            if s == nb - 1:
                group_fin("vector", *fin_items[10])
            if 2 <= s + 1 < nb:
                multiply_block(*blocks[s + 1])
            group_block(*blocks[s], 2 <= s < nb - 1)
            group_fin_at(s)
            if s == nb - 4:
                nc.scalar.copy(out=gain_f32[:], in_=gain_col[:])
        multiply_unit(0, 0)
        multiply_unit(0, 1)
        spread_gain(0)

        last = len(pairs) - 1
        for k, (n, c) in enumerate(pairs):
            first, second = 2 * c, 2 * c + 1
            before = pairs[k - 1]
            add_rest(n, first)
            if k < 2:
                quantize_block(*blocks[nb - 2 + k])
            quantize_fin_at(nb + k)
            if k >= 4:
                quantize_y(pairs[k - 4][0], (2 * pairs[k - 4][1], 2 * pairs[k - 4][1] + 1))
                if pairs[k - 4][1] == CHUNKS - 1:
                    store_codes(pairs[k - 4][0], slice(0, M))
                if pairs[k - 4] == (0, CHUNKS - 1):
                    store_scales(slice(0, 1), [nc.sync])
            weigh("gpsimd", n, first)
            if k < last:
                multiply_unit(pairs[k + 1][0], 2 * pairs[k + 1][1])
            if k >= 2:
                turn_y(pairs[k - 2][0], (2 * pairs[k - 2][1], 2 * pairs[k - 2][1] + 1))
            if k >= 1:
                round_y(before[0], 2 * before[1])
                weigh("vector", before[0], 2 * before[1] + 1)
            if k >= 1:
                round_y(before[0], 2 * before[1] + 1)
            if k >= 2:
                group_y(pairs[k - 2][0], (2 * pairs[k - 2][1], 2 * pairs[k - 2][1] + 1))
            add_rest(n, second)
            if c == 1 and n + 1 < NG:
                spread_gain(n + 1)
            if k < last:
                multiply_unit(pairs[k + 1][0], 2 * pairs[k + 1][1] + 1)
            group_fin_at(nb + k)

        n = NG - 1
        turn_y(n, (2, 3))
        weigh_and_round(n, 5)
        round_y(n, 4)
        quantize_y(n - 1, (4, 5))
        store_codes(n - 1, slice(0, M))
        quantize_y(n, (0, 1))
        group_y(n, (2, 3))
        weigh("vector", n, 5)
        store_y(n, 5)
        turn_y(n, (4, 5))
        quantize_y(n, (2, 3))
        store_codes(n, slice(0, 2 * CHUNK))
        group_y(n, (4, 5))
        quantize_y(n, (4, 5))
        store_codes(n, slice(2 * CHUNK, M))
        store_scales(slice(1, NG), [nc.scalar, nc.sync])
